import numpy as np
import ml_dtypes

BF16 = ml_dtypes.bfloat16


def bf(x):
    return np.asarray(x, np.float32).astype(BF16)


def f32(x):
    return np.asarray(x, np.float32)


def f64(x):
    return np.asarray(x).astype(np.float64)


def striped(idx):
    return np.concatenate([l.reshape(-1, 16).T for l in idx])


def rows(idx, k):
    return np.tile(np.repeat(idx, 16, axis=0), (k // (16 * 8), 1))


def look(tab, idx):
    return np.take_along_axis(f64(tab), rows(idx, len(tab)), axis=1)


K, S, D, V, N = 512, 2048, 2, 512, 1024


def setup_inputs():
    return {"tab": f32(np.random.standard_normal((K, S))), "ctr": f32(np.random.standard_normal((K, V))), "offs": striped(np.stack([np.random.permutation(S)[:N] for _ in range(8)]))}


def reference(tab, ctr, offs):
    idx = np.stack([g.T.reshape(-1) for g in np.split(offs, 8)])
    x = sum(np.maximum(look(tab, idx[:, d * V:(d + 1) * V]) - f64(ctr), 0.0) for d in range(D))
    return x

@@ -1,0 +1,44 @@
+import concourse.mybir as mybir
+
+F32, U16 = mybir.dt.float32, mybir.dt.uint16
+SUBTRACT, MAX, ADD = mybir.AluOpType.subtract, mybir.AluOpType.max, mybir.AluOpType.add
+RELU = mybir.ActivationFunctionType.Relu
+
+P = 128
+K, S, V, D = 512, 2048, 512, 2
+BLOCKS = K // P
+LIST_COLUMNS = V // 16
+FLOPS = 3 * K * V * D
+
+
+def tile_lookup_edge_sub_out_kernel(tc, tab, ctr, offs, out):
+    nc = tc.nc
+    with (
+        tc.tile_pool(name="lists", bufs=1) as lists,
+        tc.tile_pool(name="blocks", bufs=BLOCKS) as blocks,
+    ):
+        offsets = lists.tile([P, D * LIST_COLUMNS], U16, name="offsets")
+        nc.sync.dma_start(offsets[:], offs)
+        tables, centres = [], []
+        for b in range(BLOCKS):
+            rows = slice(b * P, (b + 1) * P)
+            table = blocks.tile([P, S], F32, name="table")
+            centre = blocks.tile([P, V], F32, name="centre")
+            nc.sync.dma_start(centre[:], ctr[rows, :])
+            nc.sync.dma_start(table[:], tab[rows, :])
+            tables.append(table)
+            centres.append(centre)
+
+        for b in range(BLOCKS):
+            rows = slice(b * P, (b + 1) * P)
+            first = blocks.tile([P, V], F32, name="first")
+            second = blocks.tile([P, V], F32, name="second")
+            positive = blocks.tile([P, V], F32, name="positive")
+            total = blocks.tile([P, V], F32, name="total")
+            nc.vector.tensor_tensor(
+                first[:], tables[b][:].indirect(offsets[:, 0:LIST_COLUMNS]), centres[b][:], SUBTRACT)
+            nc.vector.tensor_tensor(
+                second[:], tables[b][:].indirect(offsets[:, LIST_COLUMNS : 2 * LIST_COLUMNS]), centres[b][:], SUBTRACT)
+            nc.scalar.activation(positive[:], first[:], RELU)
+            nc.vector.scalar_tensor_tensor(total[:], second[:], 0.0, positive[:], MAX, ADD)
+            nc.sync.dma_start(out[rows, :], total[:])

@@ -1,12 +1,14 @@
 import concourse.mybir as mybir
+from concourse.masks import make_identity
 
 F32, U16 = mybir.dt.float32, mybir.dt.uint16
 SUBTRACT, MAX, ADD = mybir.AluOpType.subtract, mybir.AluOpType.max, mybir.AluOpType.add
-RELU = mybir.ActivationFunctionType.Relu
+RELU, COPY = mybir.ActivationFunctionType.Relu, mybir.ActivationFunctionType.Copy
 
 P = 128
 K, S, V, D = 512, 2048, 512, 2
 BLOCKS = K // P
+ON_TENSOR = 2
 LIST_COLUMNS = V // 16
 FLOPS = 3 * K * V * D
 
@@ -16,9 +18,12 @@ def tile_lookup_edge_sub_out_kernel(tc, tab, ctr, offs, out):
     with (
         tc.tile_pool(name="lists", bufs=1) as lists,
         tc.tile_pool(name="blocks", bufs=BLOCKS) as blocks,
+        tc.psum_pool(name="sums", bufs=2) as sums,
     ):
         offsets = lists.tile([P, D * LIST_COLUMNS], U16, name="offsets")
         nc.sync.dma_start(offsets[:], offs)
+        identity = lists.tile([P, P], F32, name="identity")
+        make_identity(nc, identity[:])
         tables, centres = [], []
         for b in range(BLOCKS):
             rows = slice(b * P, (b + 1) * P)
@@ -29,16 +34,28 @@ def tile_lookup_edge_sub_out_kernel(tc, tab, ctr, offs, out):
             tables.append(table)
             centres.append(centre)
 
+        early = lists.tile([P, ON_TENSOR, V], F32, name="early")
         for b in range(BLOCKS):
             rows = slice(b * P, (b + 1) * P)
             first = blocks.tile([P, V], F32, name="first")
             second = blocks.tile([P, V], F32, name="second")
             positive = blocks.tile([P, V], F32, name="positive")
-            total = blocks.tile([P, V], F32, name="total")
             nc.vector.tensor_tensor(
                 first[:], tables[b][:].indirect(offsets[:, 0:LIST_COLUMNS]), centres[b][:], SUBTRACT)
             nc.vector.tensor_tensor(
                 second[:], tables[b][:].indirect(offsets[:, LIST_COLUMNS : 2 * LIST_COLUMNS]), centres[b][:], SUBTRACT)
             nc.scalar.activation(positive[:], first[:], RELU)
-            nc.vector.scalar_tensor_tensor(total[:], second[:], 0.0, positive[:], MAX, ADD)
-            nc.sync.dma_start(out[rows, :], total[:])
+            if b < ON_TENSOR:
+                other = blocks.tile([P, V], F32, name="other")
+                bank = sums.tile([P, V], F32, name="bank")
+                nc.scalar.activation(other[:], second[:], RELU)
+                nc.tensor.matmul(bank[:], identity[:], positive[:], start=True, stop=False)
+                nc.tensor.matmul(bank[:], identity[:], other[:], start=False, stop=True)
+                nc.scalar.activation(early[:, b, :], bank[:], COPY)
+            else:
+                total = blocks.tile([P, V], F32, name="total")
+                nc.vector.scalar_tensor_tensor(total[:], second[:], 0.0, positive[:], MAX, ADD)
+                queue = nc.sync if b == BLOCKS - 1 else nc.scalar
+                queue.dma_start(out[rows, :], total[:])
+            if b == ON_TENSOR - 1:
+                nc.scalar.dma_start(out[0 : ON_TENSOR * P, :].rearrange("(b p) v -> p b v", p=P), early[:])

@@ -7,55 +7,68 @@ RELU, COPY = mybir.ActivationFunctionType.Relu, mybir.ActivationFunctionType.Cop
 
 P = 128
 K, S, V, D = 512, 2048, 512, 2
-BLOCKS = K // P
-ON_TENSOR = 2
 LIST_COLUMNS = V // 16
+BLOCKS = K // P
+HALF = BLOCKS // 2
+LAST_PIECES = 2
 FLOPS = 3 * K * V * D
 
 
 def tile_lookup_edge_sub_out_kernel(tc, tab, ctr, offs, out):
     nc = tc.nc
+    out_blocks = out.rearrange("(b p) v -> p b v", p=P)
     with (
-        tc.tile_pool(name="lists", bufs=1) as lists,
+        tc.tile_pool(name="held", bufs=1) as held,
         tc.tile_pool(name="blocks", bufs=BLOCKS) as blocks,
-        tc.psum_pool(name="sums", bufs=2) as sums,
+        tc.psum_pool(name="sums", bufs=HALF) as sums,
     ):
-        offsets = lists.tile([P, D * LIST_COLUMNS], U16, name="offsets")
+        offsets = held.tile([P, D * LIST_COLUMNS], U16, name="offsets")
         nc.sync.dma_start(offsets[:], offs)
-        identity = lists.tile([P, P], F32, name="identity")
-        make_identity(nc, identity[:])
         tables, centres = [], []
         for b in range(BLOCKS):
             rows = slice(b * P, (b + 1) * P)
-            table = blocks.tile([P, S], F32, name="table")
             centre = blocks.tile([P, V], F32, name="centre")
+            table = blocks.tile([P, S], F32, name="table")
             nc.sync.dma_start(centre[:], ctr[rows, :])
             nc.sync.dma_start(table[:], tab[rows, :])
-            tables.append(table)
             centres.append(centre)
+            tables.append(table)
 
-        early = lists.tile([P, ON_TENSOR, V], F32, name="early")
-        for b in range(BLOCKS):
-            rows = slice(b * P, (b + 1) * P)
+        identity = held.tile([P, P], F32, name="identity")
+        make_identity(nc, identity[:])
+
+        def look_up(b, d, difference):
+            entries = offsets[:, d * LIST_COLUMNS : (d + 1) * LIST_COLUMNS]
+            nc.vector.tensor_tensor(difference[:], tables[b][:].indirect(entries), centres[b][:], SUBTRACT)
+
+        early = held.tile([P, HALF, V], F32, name="early")
+        for b in range(HALF):
             first = blocks.tile([P, V], F32, name="first")
             second = blocks.tile([P, V], F32, name="second")
-            positive = blocks.tile([P, V], F32, name="positive")
-            nc.vector.tensor_tensor(
-                first[:], tables[b][:].indirect(offsets[:, 0:LIST_COLUMNS]), centres[b][:], SUBTRACT)
-            nc.vector.tensor_tensor(
-                second[:], tables[b][:].indirect(offsets[:, LIST_COLUMNS : 2 * LIST_COLUMNS]), centres[b][:], SUBTRACT)
-            nc.scalar.activation(positive[:], first[:], RELU)
-            if b < ON_TENSOR:
-                other = blocks.tile([P, V], F32, name="other")
-                bank = sums.tile([P, V], F32, name="bank")
-                nc.scalar.activation(other[:], second[:], RELU)
-                nc.tensor.matmul(bank[:], identity[:], positive[:], start=True, stop=False)
-                nc.tensor.matmul(bank[:], identity[:], other[:], start=False, stop=True)
-                nc.scalar.activation(early[:, b, :], bank[:], COPY)
-            else:
-                total = blocks.tile([P, V], F32, name="total")
-                nc.vector.scalar_tensor_tensor(total[:], second[:], 0.0, positive[:], MAX, ADD)
-                queue = nc.sync if b == BLOCKS - 1 else nc.scalar
-                queue.dma_start(out[rows, :], total[:])
-            if b == ON_TENSOR - 1:
-                nc.scalar.dma_start(out[0 : ON_TENSOR * P, :].rearrange("(b p) v -> p b v", p=P), early[:])
+            first_part = blocks.tile([P, V], F32, name="first_part")
+            second_part = blocks.tile([P, V], F32, name="second_part")
+            total = sums.tile([P, V], F32, name="total")
+            look_up(b, 0, first)
+            look_up(b, 1, second)
+            nc.scalar.activation(first_part[:], first[:], RELU)
+            nc.scalar.activation(second_part[:], second[:], RELU)
+            nc.tensor.matmul(total[:], identity[:], first_part[:], start=True, stop=False)
+            nc.tensor.matmul(total[:], identity[:], second_part[:], start=False, stop=True)
+            nc.scalar.activation(early[:, b, :], total[:], COPY)
+        nc.scalar.dma_start(out_blocks[:, 0:HALF, :], early[:])
+
+        for b in range(HALF, BLOCKS):
+            first = blocks.tile([P, V], F32, name="first")
+            second = blocks.tile([P, V], F32, name="second")
+            first_part = blocks.tile([P, V], F32, name="first_part")
+            result = blocks.tile([P, V], F32, name="result")
+            look_up(b, 0, first)
+            look_up(b, 1, second)
+            nc.scalar.activation(first_part[:], first[:], RELU)
+            last = b == BLOCKS - 1
+            pieces = LAST_PIECES if last else 1
+            queue = nc.sync if last else nc.scalar
+            for i in range(pieces):
+                piece = slice(i * V // pieces, (i + 1) * V // pieces)
+                nc.vector.scalar_tensor_tensor(result[:, piece], second[:, piece], 0.0, first_part[:, piece], MAX, ADD)
+                queue.dma_start(out_blocks[:, b, piece], result[:, piece])

import concourse.mybir as mybir
from concourse.masks import make_identity

F32, U16 = mybir.dt.float32, mybir.dt.uint16
SUBTRACT, MAX, ADD = mybir.AluOpType.subtract, mybir.AluOpType.max, mybir.AluOpType.add
RELU, COPY = mybir.ActivationFunctionType.Relu, mybir.ActivationFunctionType.Copy

P = 128
K, S, V, D = 512, 2048, 512, 2
LIST_COLUMNS = V // 16
BLOCKS = K // P
HALF = BLOCKS // 2
LAST_PIECES = 2
FLOPS = 3 * K * V * D


def tile_lookup_edge_sub_out_kernel(tc, tab, ctr, offs, out):
    nc = tc.nc
    out_blocks = out.rearrange("(b p) v -> p b v", p=P)
    with (
        tc.tile_pool(name="held", bufs=1) as held,
        tc.tile_pool(name="blocks", bufs=BLOCKS) as blocks,
        tc.psum_pool(name="sums", bufs=HALF) as sums,
    ):
        offsets = held.tile([P, D * LIST_COLUMNS], U16, name="offsets")
        nc.sync.dma_start(offsets[:], offs)
        tables, centres = [], []
        for b in range(BLOCKS):
            rows = slice(b * P, (b + 1) * P)
            centre = blocks.tile([P, V], F32, name="centre")
            table = blocks.tile([P, S], F32, name="table")
            nc.sync.dma_start(centre[:], ctr[rows, :])
            nc.sync.dma_start(table[:], tab[rows, :])
            centres.append(centre)
            tables.append(table)

        identity = held.tile([P, P], F32, name="identity")
        make_identity(nc, identity[:])

        def look_up(b, d, difference):
            entries = offsets[:, d * LIST_COLUMNS : (d + 1) * LIST_COLUMNS]
            nc.vector.tensor_tensor(difference[:], tables[b][:].indirect(entries), centres[b][:], SUBTRACT)

        early = held.tile([P, HALF, V], F32, name="early")
        for b in range(HALF):
            first = blocks.tile([P, V], F32, name="first")
            second = blocks.tile([P, V], F32, name="second")
            first_part = blocks.tile([P, V], F32, name="first_part")
            second_part = blocks.tile([P, V], F32, name="second_part")
            total = sums.tile([P, V], F32, name="total")
            look_up(b, 0, first)
            look_up(b, 1, second)
            nc.scalar.activation(first_part[:], first[:], RELU)
            nc.scalar.activation(second_part[:], second[:], RELU)
            nc.tensor.matmul(total[:], identity[:], first_part[:], start=True, stop=False)
            nc.tensor.matmul(total[:], identity[:], second_part[:], start=False, stop=True)
            nc.scalar.activation(early[:, b, :], total[:], COPY)
        nc.scalar.dma_start(out_blocks[:, 0:HALF, :], early[:])

        for b in range(HALF, BLOCKS):
            first = blocks.tile([P, V], F32, name="first")
            second = blocks.tile([P, V], F32, name="second")
            first_part = blocks.tile([P, V], F32, name="first_part")
            result = blocks.tile([P, V], F32, name="result")
            look_up(b, 0, first)
            look_up(b, 1, second)
            nc.scalar.activation(first_part[:], first[:], RELU)
            last = b == BLOCKS - 1
            pieces = LAST_PIECES if last else 1
            queue = nc.sync if last else nc.scalar
            for i in range(pieces):
                piece = slice(i * V // pieces, (i + 1) * V // pieces)
                nc.vector.scalar_tensor_tensor(result[:, piece], second[:, piece], 0.0, first_part[:, piece], MAX, ADD)
                queue.dma_start(out_blocks[:, b, piece], result[:, piece])
